import numpy as np
import ml_dtypes


def mxq(x, axis, fmt="e4m3"):
    dtype, down = {"e4m3": (ml_dtypes.float8_e4m3fn, 7), "e5m2": (ml_dtypes.float8_e5m2, 14)}[fmt]
    v = np.moveaxis(np.asarray(x, np.float32).astype(ml_dtypes.bfloat16).astype(np.float64), axis, -1)
    blocks = v.reshape(v.shape[:-1] + (-1, 32))
    amax = np.abs(blocks).max(-1, keepdims=True)
    byte = np.maximum(np.where(amax > 0, np.frexp(amax)[1] - 1 + 127, 0) - down, 1)
    scale = np.exp2(byte - 127.0)
    codes = (blocks / scale).astype(np.float32).astype(dtype).astype(np.float64)
    return np.moveaxis((codes * scale).reshape(v.shape), -1, axis)


WIDE = False


def mx_kscale(k):
    if not WIDE:
        return np.ones(k)
    levels = np.array([10, -10, 5, -5, 0])
    if k % 512:
        return np.exp2(np.random.permutation(np.resize(levels, k // 32))).repeat(32)
    a = np.empty((k // 512, 16))
    for p in range(k // 512):
        a[p, :8] = np.random.permutation(np.resize(levels, 8))
        for g in range(8):
            far = levels[np.abs(levels - a[p, g]) >= 10]
            a[p, g + 8] = far[np.random.randint(len(far))]
    return np.exp2(a.ravel()).repeat(32)


def f64(x):
    return np.asarray(x).astype(np.float64)


def striped(idx):
    return np.tile(np.asarray(idx).reshape(-1, 16).T, (8, 1)).astype(np.uint16)


def unstriped(offs):
    return offs[:16].T.reshape(-1).astype(np.int64)


E2M1 = np.array([0.0, 0.5, 1.0, 1.5, 2.0, 3.0, 4.0, 6.0, -0.0, -0.5, -1.0, -1.5, -2.0, -3.0, -4.0, -6.0])


def pack_weight(w, fmt):
    k, n = w.shape
    w = f64(np.asarray(w, np.float32).astype(ml_dtypes.bfloat16)).reshape(k // 32, 32, n)
    amax = np.abs(w).max(1)
    if fmt == "e4m3":
        byte = np.frexp(amax)[1] - 1 + 127 - 7
    else:
        mant, ex = np.frexp(amax / 6.0)
        byte = np.where(mant > 0.5, ex, ex - 1) + 127
    byte = np.clip(np.where(amax > 0, byte, 1), 1, 254)
    scaled = (w * np.exp2(127.0 - byte)[:, None, :]).reshape(k, n).astype(np.float32)
    by_word = np.ascontiguousarray(scaled.reshape(k // 512, 128, 4, n).transpose(0, 1, 3, 2))
    if fmt == "e4m3":
        words = by_word.astype(ml_dtypes.float8_e4m3fn).view(np.uint8)
    else:
        c = by_word.astype(ml_dtypes.float4_e2m1fn).view(np.uint8) & 0xF
        words = (c[..., 0::2] | (c[..., 1::2] << 4)).reshape(k // 512, 128, 2 * n)
    return np.ascontiguousarray(words), np.ascontiguousarray(byte.astype(np.uint8).reshape(k // 512, 16, n))


def unpack_weight(words, scales, fmt):
    g, _, n = scales.shape
    words = np.ascontiguousarray(words).reshape(g, 128, n, -1)
    if fmt == "e4m3":
        vals = words.view(ml_dtypes.float8_e4m3fn).astype(np.float64)
    else:
        nib = np.empty((g, 128, n, 4), np.uint8)
        nib[..., 0::2] = words & 0xF
        nib[..., 1::2] = words >> 4
        vals = E2M1[nib]
    vals = vals * np.repeat(np.exp2(scales.astype(np.float64) - 127.0), 8, axis=1)[..., None]
    return vals.transpose(0, 1, 3, 2).reshape(g * 512, n)


B, N, T, D, DV, NQ = 1, 512, 1024, 1024, 256, 256


def setup_inputs():
    n = np.random.standard_normal
    idx = np.sort(np.random.permutation(T)[:B * N].reshape(B, N), axis=1).reshape(-1)
    s = mx_kscale(D)[:, None]
    u = np.ones(T)
    u[idx] = mx_kscale(B * N)
    r = np.random.uniform(0.5, 2.0, T)
    k = n((D, T)) / s
    v = n((DV, T)) / (u * r)
    kp = pack_weight(k, "e2m1")
    return {
        "qT": (n((B, D, NQ)) * s * (0.80 / np.sqrt(D))).astype(np.float32),
        "k_words": np.ascontiguousarray(kp[0].reshape(D // 1024, 2, 128, T, 2).transpose(0, 2, 3, 1, 4)).reshape(D // 1024, 128, T, 4),
        "k_scales": kp[1],
        "vT": v.astype(np.float32),
        "vs": np.tile(u * r, (128, 1)).astype(np.float32),
        "sink": (2.0 + 3.0 * n((B, NQ, 1))).astype(np.float32),
        "og": n((B, NQ, DV)).astype(np.float32),
        "offs": striped(idx),
    }


def reference(qT, k_words, k_scales, vT, vs, sink, og, offs):
    idx = unstriped(offs)
    k = unpack_weight(k_words.reshape(D // 1024, 128, T, 2, 2).transpose(0, 3, 1, 2, 4).reshape(D // 512, 128, 2 * T), k_scales, "e2m1")
    v = f64(vT)
    pick = lambda x: x[:, idx].reshape(x.shape[0], B, N).transpose(1, 0, 2)
    q = f64(qT)
    score = mxq(q, 1, "e4m3").transpose(0, 2, 1) @ pick(k)
    m = np.maximum(score.max(-1, keepdims=True), f64(sink))
    p = np.exp(score - m)
    total = p.sum(-1, keepdims=True) + np.exp(f64(sink) - m)
    w = p * pick(f64(vs))[:, :1, :]
    y = mxq(w, 2, "e4m3") @ mxq(pick(v).transpose(0, 2, 1), 1, "e4m3")
    y = y / total
    y = y / (1.0 + np.exp(-f64(og)))
    return y

@@ -1,0 +1,173 @@
+from contextlib import ExitStack
+
+import concourse.mybir as mybir
+from concourse.masks import make_identity
+
+F32 = mybir.dt.float32
+BF16 = mybir.dt.bfloat16
+I32 = mybir.dt.int32
+U32 = mybir.dt.uint32
+U16 = mybir.dt.uint16
+U8 = mybir.dt.uint8
+FP8X4 = mybir.dt.float8_e4m3fn_x4
+FP4X4 = mybir.dt.float4_e2m1fn_x4
+ACT = mybir.ActivationFunctionType
+ALU = mybir.AluOpType
+
+N, T, D, DV, NQ = 512, 1024, 1024, 256, 256
+P = 128
+PACK = 4
+PASSES = D // (P * PACK)
+QBLOCKS = NQ // P
+VHALVES = DV // P
+SCALE_ROWS = 16
+QUADS = 4
+
+FLOPS = 2 * NQ * N * (D + DV)
+
+
+def tile_attend_soft_sink_gate_srtq256n512t1024_kernel(tc, qT, k_words, k_scales, vT, vs, sink, og, offs, out):
+    nc = tc.nc
+    with ExitStack() as ctx:
+        sb = ctx.enter_context(tc.tile_pool(name="sb", bufs=1))
+        ps = ctx.enter_context(tc.psum_pool(name="ps", bufs=1))
+
+        offsets = sb.tile([P, N // 16], U16, name="offsets")
+        nc.sync.dma_start(offsets[:], offs)
+        sink_cols = sb.tile([P, QBLOCKS], F32, name="sink_cols")
+        with nc.allow_non_contiguous_dma(reason="one logit a partition"):
+            nc.scalar.dma_start(sink_cols[:], sink[0].rearrange("(b p) o -> p (b o)", p=P))
+        first_row = P - PASSES * SCALE_ROWS
+        ks_pool = sb.tile([P, T], U8, name="ks_pool", tag="pool0")
+        nc.vector.memset(ks_pool[:first_row, :].bitcast(I32), 0)
+        nc.sync.dma_start(ks_pool[first_row:, :].bitcast(I32), k_scales.bitcast(I32).rearrange("o f t -> f o t"))
+        vs_pool = sb.tile([P, T], F32, name="vs_pool", tag="pool1")
+        nc.vector.memset(vs_pool[: P - 1, :], 0.0)
+        nc.sync.dma_start(vs_pool[P - 1 :, :], vs[0:1, :])
+        kw_pool = sb.tile([P, T], U32, name="kw_pool", tag="pool2")
+        nc.sync.dma_start(kw_pool[:].bitcast(I32), k_words[0].rearrange("p t b -> p (t b)").bitcast(I32))
+        q_raw = []
+        for g in range(PASSES):
+            t_ = sb.tile([P, PACK, NQ], F32, name=f"q_raw{g}")
+            nc.sync.dma_start(t_[:], qT[0, g * P * PACK : (g + 1) * P * PACK, :].rearrange("(p j) q -> p j q", j=PACK))
+            q_raw.append(t_)
+        k_scale = sb.tile([P, PASSES, N], U8, name="k_scale", align_bytes=64)
+        nc.gpsimd.memset(k_scale[:].rearrange("p o n -> p (o n)").bitcast(I32), 0)
+        ident = sb.tile([P, P], F32, name="ident")
+        make_identity(nc, ident[:])
+
+        neg_score, neg_sink = [], []
+        for b in range(QBLOCKS):
+            t_ = sb.tile([P, N + 1], F32, name=f"neg_score{b}")
+            nc.scalar.activation(t_[:, N : N + 1], sink_cols[:, b : b + 1], ACT.Copy, scale=-1.0)
+            neg_score.append(t_)
+            t_ = sb.tile([P, 1], F32, name=f"neg_sink{b}", tag=f"late{b}")
+            nc.scalar.activation(t_[:], sink_cols[:, b : b + 1], ACT.Copy, scale=-1.0)
+            neg_sink.append(t_)
+
+        ks_got = sb.tile([P, N], U8, name="ks_got")
+        nc.vector.tensor_copy(ks_got[:], ks_pool[:].indirect(offsets[:]))
+        rows = PASSES * SCALE_ROWS // QUADS
+        for quad in range(QUADS):
+            nc.sync.dma_start(
+                k_scale[32 * quad : 32 * quad + 4, :, :].bitcast(I32),
+                ks_got[first_row + rows * quad : first_row + rows * (quad + 1), :].bitcast(I32),
+            )
+        vs_got = sb.tile([P, N], F32, name="vs_got")
+        nc.vector.tensor_copy(vs_got[:], vs_pool[:].indirect(offsets[:]))
+        vs_turned = ps.tile([P, PACK, P], F32, name="vs_turned", tag="y1")
+        for t in range(PACK):
+            nc.tensor.transpose(vs_turned[:, t, :], vs_got[:, t::PACK], ident[:])
+        vs_col = sb.tile([P, PACK], F32, name="vs_col")
+
+        kw_got = sb.tile([P, N], U32, name="kw_got")
+        nc.vector.tensor_copy(kw_got[:], kw_pool[:].indirect(offsets[:]))
+        k_code = sb.tile([P, PASSES, 2 * N], U8, name="k_code", align_bytes=64)
+        nc.vector.tensor_copy(k_code[:].bitcast(U16), kw_got[:].bitcast(U16).rearrange("p (n o) -> p o n", o=PASSES))
+
+        v_pool = []
+        for h in range(VHALVES):
+            t_ = sb.tile([P, T], F32, name=f"v_pool{h}", tag=f"pool{h}")
+            nc.sync.dma_start(t_[:], vT[h * P : (h + 1) * P, :])
+            v_pool.append(t_)
+        og_sb = sb.tile([P, QBLOCKS, DV], F32, name="og_sb", tag="pool2")
+        nc.sync.dma_start(og_sb[:], og[0].rearrange("(b p) e -> p b e", p=P))
+
+        q_code, q_scale = {}, {}
+        for g in range(PASSES):
+            for b in range(QBLOCKS):
+                woven = sb.tile([P, P, PACK], BF16, name=f"q_woven{g}{b}", align_bytes=64)
+                nc.scalar.activation(
+                    woven[:].rearrange("p (c i) t -> p c t i", i=4),
+                    q_raw[g][:, :, b * P : (b + 1) * P].rearrange("p t (c i) -> p c t i", i=4),
+                    ACT.Copy,
+                )
+                q_code[g, b] = sb.tile([P, P], U32, name=f"q_code{g}{b}", align_bytes=64)
+                q_scale[g, b] = sb.tile([P, P], U8, name=f"q_scale{g}{b}", align_bytes=64)
+                nc.vector.quantize_mx(q_code[g, b][:].bitcast(FP8X4), q_scale[g, b][:], woven[:].rearrange("p c t -> p (c t)"))
+        nc.scalar.copy(vs_col[:], vs_turned[:, :, P - 1])
+
+        p_turned, total = [], []
+        for b in range(QBLOCKS):
+            score = ps.tile([P, N], F32, name=f"score{b}")
+            for g in range(PASSES):
+                nc.tensor.matmul_mx(
+                    score[:], lhsT=q_code[g, b][:].bitcast(FP8X4), lhsT_scale=q_scale[g, b][:],
+                    rhs=k_code[:, g, :].bitcast(FP4X4), rhs_scale=k_scale[:, g, :],
+                    start=(g == 0), stop=(g == PASSES - 1),
+                )
+            neg_max = sb.tile([P, 1], F32, name=f"neg_max{b}")
+            nc.vector.tensor_scalar(
+                neg_score[b][:, :N].rearrange("q (t s) -> q t s", t=PACK),
+                score[:].rearrange("q (s t) -> q t s", t=PACK),
+                -1.0, neg_sink[b][:], ALU.mult, ALU.min, accum_out=neg_max[:],
+            )
+            prob = sb.tile([P, N + 1], F32, name=f"prob{b}")
+            tot = sb.tile([P, 1], F32, name=f"total{b}")
+            nc.scalar.activation(prob[:], neg_score[b][:], ACT.Exp, bias=neg_max[:], scale=-1.0, accum_out=tot[:])
+            turned = ps.tile([P, PACK, P], F32, name=f"p_turned{b}")
+            for t in range(PACK):
+                nc.tensor.transpose(turned[:, t, :], prob[:, t * P : (t + 1) * P], ident[:])
+            p_turned.append(turned)
+            total.append(tot)
+
+        v_code = sb.tile([P, DV], U32, name="v_code", align_bytes=64)
+        v_scale = sb.tile([P, DV], U8, name="v_scale", align_bytes=64)
+        for h in range(VHALVES):
+            v_got = sb.tile([P, N], BF16, name=f"v_got{h}", tag=f"late{h}")
+            nc.vector.tensor_copy(v_got[:], v_pool[h][:].indirect(offsets[:]))
+            v_turned = ps.tile([P, 2, P], F32, name=f"v_turned{h}")
+            pairs = v_got[:].bitcast(F32)
+            for u in range(2):
+                nc.tensor.transpose(v_turned[:, u, :], pairs[:, u::2], ident[:])
+            v_woven = sb.tile([P, P, PACK], BF16, name=f"v_woven{h}", align_bytes=64)
+            nc.scalar.copy(v_woven[:].bitcast(F32), v_turned[:].rearrange("s u e -> s e u"))
+            nc.vector.quantize_mx(
+                v_code[:, h * P : (h + 1) * P].bitcast(FP8X4), v_scale[:, h * P : (h + 1) * P],
+                v_woven[:].rearrange("s e t -> s (e t)"),
+            )
+
+        half_tanh = sb.tile([P, QBLOCKS, DV], F32, name="half_tanh")
+        nc.scalar.activation(half_tanh[:], og_sb[:], ACT.Tanh, scale=0.5)
+        gate = sb.tile([P, QBLOCKS, DV], F32, name="gate")
+        nc.scalar.activation(gate[:], half_tanh[:], ACT.Copy, scale=0.5, bias=0.5)
+
+        for b in range(QBLOCKS):
+            w_woven = sb.tile([P, P, PACK], BF16, name=f"w_woven{b}", align_bytes=64)
+            nc.vector.tensor_tensor(
+                w_woven[:], p_turned[b][:].rearrange("s t q -> s q t"),
+                vs_col[:].unsqueeze(1).to_broadcast([P, P, PACK]), ALU.mult,
+            )
+            inv_total = sb.tile([P, 1], F32, name=f"inv_total{b}")
+            nc.vector.reciprocal(inv_total[:], total[b][:])
+            w_code = sb.tile([P, P], U32, name=f"w_code{b}", align_bytes=64)
+            w_scale = sb.tile([P, P], U8, name=f"w_scale{b}", align_bytes=64)
+            nc.vector.quantize_mx(w_code[:].bitcast(FP8X4), w_scale[:], w_woven[:].rearrange("s q t -> s (q t)"))
+            y = ps.tile([P, DV], F32, name=f"y{b}", tag=f"y{b}")
+            nc.tensor.matmul_mx(
+                y[:], lhsT=w_code[:].bitcast(FP8X4), lhsT_scale=w_scale[:],
+                rhs=v_code[:].bitcast(FP8X4), rhs_scale=v_scale[:], start=True, stop=True,
+            )
+            result = sb.tile([P, DV], F32, name=f"result{b}")
+            nc.vector.scalar_tensor_tensor(result[:], y[:], inv_total[:], gate[:, b, :], ALU.mult, ALU.mult)
+            nc.sync.dma_start(out[0, b * P : (b + 1) * P, :], result[:])

@@ -34,21 +34,21 @@ def tile_attend_soft_sink_gate_srtq256n512t1024_kernel(tc, qT, k_words, k_scales
 
         offsets = sb.tile([P, N // 16], U16, name="offsets")
         nc.sync.dma_start(offsets[:], offs)
-        sink_cols = sb.tile([P, QBLOCKS], F32, name="sink_cols")
-        with nc.allow_non_contiguous_dma(reason="one logit a partition"):
-            nc.scalar.dma_start(sink_cols[:], sink[0].rearrange("(b p) o -> p (b o)", p=P))
+        sink_rows = sb.tile([P, P], F32, name="sink_rows")
+        nc.gpsimd.memset(sink_rows[: P - QBLOCKS, :], 0.0)
+        nc.scalar.dma_start(sink_rows[P - QBLOCKS :, :], sink[0].rearrange("(b p) o -> b (p o)", p=P))
         first_row = P - PASSES * SCALE_ROWS
-        ks_pool = sb.tile([P, T], U8, name="ks_pool", tag="pool0")
+        ks_pool = sb.tile([P, T], U8, name="ks_pool", tag="pool0", align_bytes=64)
         nc.vector.memset(ks_pool[:first_row, :].bitcast(I32), 0)
         nc.sync.dma_start(ks_pool[first_row:, :].bitcast(I32), k_scales.bitcast(I32).rearrange("o f t -> f o t"))
-        vs_pool = sb.tile([P, T], F32, name="vs_pool", tag="pool1")
+        vs_pool = sb.tile([P, T], F32, name="vs_pool", tag="pool1", align_bytes=64)
         nc.vector.memset(vs_pool[: P - 1, :], 0.0)
         nc.sync.dma_start(vs_pool[P - 1 :, :], vs[0:1, :])
         kw_pool = sb.tile([P, T], U32, name="kw_pool", tag="pool2")
         nc.sync.dma_start(kw_pool[:].bitcast(I32), k_words[0].rearrange("p t b -> p (t b)").bitcast(I32))
         q_raw = []
         for g in range(PASSES):
-            t_ = sb.tile([P, PACK, NQ], F32, name=f"q_raw{g}")
+            t_ = sb.tile([P, PACK, NQ], F32, name=f"q_raw{g}", tag=f"raw{g}", align_bytes=64)
             nc.sync.dma_start(t_[:], qT[0, g * P * PACK : (g + 1) * P * PACK, :].rearrange("(p j) q -> p j q", j=PACK))
             q_raw.append(t_)
         k_scale = sb.tile([P, PASSES, N], U8, name="k_scale", align_bytes=64)
@@ -56,14 +56,20 @@ def tile_attend_soft_sink_gate_srtq256n512t1024_kernel(tc, qT, k_words, k_scales
         ident = sb.tile([P, P], F32, name="ident")
         make_identity(nc, ident[:])
 
+        sink_turned = ps.tile([P, P], F32, name="sink_turned", tag="y0")
+        nc.tensor.transpose(sink_turned[:], sink_rows[:], ident[:])
+        sink_cols = sink_turned[:, P - QBLOCKS :]
+        shared = sb.tile([P, 2 * N], BF16, name="shared", align_bytes=64)
         neg_score, neg_sink = [], []
         for b in range(QBLOCKS):
-            t_ = sb.tile([P, N + 1], F32, name=f"neg_score{b}")
+            t_ = sb.tile([P, N + 1], F32, name=f"neg_score{b}", tag=f"neg_score{b}", align_bytes=64)
             nc.scalar.activation(t_[:, N : N + 1], sink_cols[:, b : b + 1], ACT.Copy, scale=-1.0)
             neg_score.append(t_)
-            t_ = sb.tile([P, 1], F32, name=f"neg_sink{b}", tag=f"late{b}")
-            nc.scalar.activation(t_[:], sink_cols[:, b : b + 1], ACT.Copy, scale=-1.0)
-            neg_sink.append(t_)
+            if b == 0:
+                neg_sink.append(t_[:, N : N + 1])
+            else:
+                neg_sink.append(shared[:, N : N + 2].bitcast(F32))
+                nc.scalar.activation(neg_sink[b], sink_cols[:, b : b + 1], ACT.Copy, scale=-1.0)
 
         ks_got = sb.tile([P, N], U8, name="ks_got")
         nc.vector.tensor_copy(ks_got[:], ks_pool[:].indirect(offsets[:]))
@@ -78,8 +84,6 @@ def tile_attend_soft_sink_gate_srtq256n512t1024_kernel(tc, qT, k_words, k_scales
         vs_turned = ps.tile([P, PACK, P], F32, name="vs_turned", tag="y1")
         for t in range(PACK):
             nc.tensor.transpose(vs_turned[:, t, :], vs_got[:, t::PACK], ident[:])
-        vs_col = sb.tile([P, PACK], F32, name="vs_col")
-
         kw_got = sb.tile([P, N], U32, name="kw_got")
         nc.vector.tensor_copy(kw_got[:], kw_pool[:].indirect(offsets[:]))
         k_code = sb.tile([P, PASSES, 2 * N], U8, name="k_code", align_bytes=64)
@@ -87,29 +91,36 @@ def tile_attend_soft_sink_gate_srtq256n512t1024_kernel(tc, qT, k_words, k_scales
 
         v_pool = []
         for h in range(VHALVES):
-            t_ = sb.tile([P, T], F32, name=f"v_pool{h}", tag=f"pool{h}")
+            t_ = sb.tile([P, T], F32, name=f"v_pool{h}", tag=f"pool{h}", align_bytes=64)
             nc.sync.dma_start(t_[:], vT[h * P : (h + 1) * P, :])
             v_pool.append(t_)
-        og_sb = sb.tile([P, QBLOCKS, DV], F32, name="og_sb", tag="pool2")
-        nc.sync.dma_start(og_sb[:], og[0].rearrange("(b p) e -> p b e", p=P))
 
-        q_code, q_scale = {}, {}
+        q_woven, q_code, q_scale = {}, {}, {}
         for g in range(PASSES):
             for b in range(QBLOCKS):
-                woven = sb.tile([P, P, PACK], BF16, name=f"q_woven{g}{b}", align_bytes=64)
+                if (g, b) == (1, 1):
+                    q_woven[g, b] = shared[:, :N]
+                else:
+                    q_woven[g, b] = sb.tile([P, N], BF16, name=f"q_woven{g}{b}", align_bytes=64)[:]
                 nc.scalar.activation(
-                    woven[:].rearrange("p (c i) t -> p c t i", i=4),
+                    q_woven[g, b].rearrange("p (c i t) -> p c t i", i=4, t=PACK),
                     q_raw[g][:, :, b * P : (b + 1) * P].rearrange("p t (c i) -> p c t i", i=4),
                     ACT.Copy,
                 )
+        for b in range(QBLOCKS):
+            for g in range(PASSES):
                 q_code[g, b] = sb.tile([P, P], U32, name=f"q_code{g}{b}", align_bytes=64)
                 q_scale[g, b] = sb.tile([P, P], U8, name=f"q_scale{g}{b}", align_bytes=64)
-                nc.vector.quantize_mx(q_code[g, b][:].bitcast(FP8X4), q_scale[g, b][:], woven[:].rearrange("p c t -> p (c t)"))
+                nc.vector.quantize_mx(q_code[g, b][:].bitcast(FP8X4), q_scale[g, b][:], q_woven[g, b])
+        vs_col = sb.tile([P, PACK], F32, name="vs_col")
         nc.scalar.copy(vs_col[:], vs_turned[:, :, P - 1])
+        og_sb = sb.tile([P, QBLOCKS, DV], F32, name="og_sb", tag="pool2")
+        nc.sync.dma_start(og_sb[:], og[0].rearrange("(b p) e -> p b e", p=P))
 
-        p_turned, total = [], []
+        p_turned = []
+        total = sb.tile([P, QBLOCKS], F32, name="total")
         for b in range(QBLOCKS):
-            score = ps.tile([P, N], F32, name=f"score{b}")
+            score = ps.tile([P, N], F32, name=f"score{b}", tag=f"score{b}")
             for g in range(PASSES):
                 nc.tensor.matmul_mx(
                     score[:], lhsT=q_code[g, b][:].bitcast(FP8X4), lhsT_scale=q_scale[g, b][:],
@@ -120,54 +131,68 @@ def tile_attend_soft_sink_gate_srtq256n512t1024_kernel(tc, qT, k_words, k_scales
             nc.vector.tensor_scalar(
                 neg_score[b][:, :N].rearrange("q (t s) -> q t s", t=PACK),
                 score[:].rearrange("q (s t) -> q t s", t=PACK),
-                -1.0, neg_sink[b][:], ALU.mult, ALU.min, accum_out=neg_max[:],
+                -1.0, neg_sink[b], ALU.mult, ALU.min, accum_out=neg_max[:],
             )
             prob = sb.tile([P, N + 1], F32, name=f"prob{b}")
-            tot = sb.tile([P, 1], F32, name=f"total{b}")
-            nc.scalar.activation(prob[:], neg_score[b][:], ACT.Exp, bias=neg_max[:], scale=-1.0, accum_out=tot[:])
+            nc.scalar.activation(prob[:], neg_score[b][:], ACT.Exp, bias=neg_max[:], scale=-1.0, accum_out=total[:, b : b + 1])
             turned = ps.tile([P, PACK, P], F32, name=f"p_turned{b}")
             for t in range(PACK):
                 nc.tensor.transpose(turned[:, t, :], prob[:, t * P : (t + 1) * P], ident[:])
             p_turned.append(turned)
-            total.append(tot)
 
-        v_code = sb.tile([P, DV], U32, name="v_code", align_bytes=64)
-        v_scale = sb.tile([P, DV], U8, name="v_scale", align_bytes=64)
-        for h in range(VHALVES):
-            v_got = sb.tile([P, N], BF16, name=f"v_got{h}", tag=f"late{h}")
-            nc.vector.tensor_copy(v_got[:], v_pool[h][:].indirect(offsets[:]))
-            v_turned = ps.tile([P, 2, P], F32, name=f"v_turned{h}")
-            pairs = v_got[:].bitcast(F32)
-            for u in range(2):
-                nc.tensor.transpose(v_turned[:, u, :], pairs[:, u::2], ident[:])
-            v_woven = sb.tile([P, P, PACK], BF16, name=f"v_woven{h}", align_bytes=64)
-            nc.scalar.copy(v_woven[:].bitcast(F32), v_turned[:].rearrange("s u e -> s e u"))
-            nc.vector.quantize_mx(
-                v_code[:, h * P : (h + 1) * P].bitcast(FP8X4), v_scale[:, h * P : (h + 1) * P],
-                v_woven[:].rearrange("s e t -> s (e t)"),
-            )
 
-        half_tanh = sb.tile([P, QBLOCKS, DV], F32, name="half_tanh")
+        half_tanh = sb.tile([P, QBLOCKS, DV], F32, name="half_tanh", tag="neg_score1", align_bytes=64)
         nc.scalar.activation(half_tanh[:], og_sb[:], ACT.Tanh, scale=0.5)
         gate = sb.tile([P, QBLOCKS, DV], F32, name="gate")
         nc.scalar.activation(gate[:], half_tanh[:], ACT.Copy, scale=0.5, bias=0.5)
 
+        v_wovens = []
+        for h in (0, 1):
+            if h == 0:
+                v_got = shared[:, N // 2 : N // 2 + N]
+                for part in range(2):
+                    nc.vector.tensor_copy(v_got[:, part * 256 : (part + 1) * 256], v_pool[h][:].indirect(offsets[:, 16 * part : 16 * (part + 1)]))
+            else:
+                v_got = sb.tile([P, N], BF16, name=f"v_got{h}", tag="pool0", align_bytes=64)[:]
+                nc.vector.tensor_copy(v_got, v_pool[h][:].indirect(offsets[:]))
+            v_turned = ps.tile([P, 2, P], F32, name=f"v_turned{h}")
+            pairs = v_got.bitcast(F32)
+            for u in range(2):
+                nc.tensor.transpose(v_turned[:, u, :], pairs[:, u::2], ident[:])
+            v_woven = sb.tile([P, P, PACK], BF16, name=f"v_woven{h}", tag=("neg_score1", "vwoven1")[h], align_bytes=64)
+            nc.scalar.copy(v_woven[:].bitcast(F32), v_turned[:].rearrange("s u e -> s e u"))
+            v_wovens.append(v_woven)
+
+        v_code = sb.tile([P, DV], U32, name="v_code", align_bytes=64)
+        v_scale = sb.tile([P, DV], U8, name="v_scale", align_bytes=64)
+        inv_total = sb.tile([P, QBLOCKS], F32, name="inv_total")
+
+        def quantise_values(h):
+            nc.vector.quantize_mx(
+                v_code[:, h * P : (h + 1) * P].bitcast(FP8X4), v_scale[:, h * P : (h + 1) * P],
+                v_wovens[h][:].rearrange("s e t -> s (e t)"),
+            )
+
+        y, w_code, w_scale = [], [], []
         for b in range(QBLOCKS):
-            w_woven = sb.tile([P, P, PACK], BF16, name=f"w_woven{b}", align_bytes=64)
+            w_woven = sb.tile([P, P, PACK], BF16, name=f"w_woven{b}", tag=("pool1", "wwoven1")[b], align_bytes=64)
             nc.vector.tensor_tensor(
                 w_woven[:], p_turned[b][:].rearrange("s t q -> s q t"),
                 vs_col[:].unsqueeze(1).to_broadcast([P, P, PACK]), ALU.mult,
             )
-            inv_total = sb.tile([P, 1], F32, name=f"inv_total{b}")
-            nc.vector.reciprocal(inv_total[:], total[b][:])
-            w_code = sb.tile([P, P], U32, name=f"w_code{b}", align_bytes=64)
-            w_scale = sb.tile([P, P], U8, name=f"w_scale{b}", align_bytes=64)
-            nc.vector.quantize_mx(w_code[:].bitcast(FP8X4), w_scale[:], w_woven[:].rearrange("s q t -> s (q t)"))
-            y = ps.tile([P, DV], F32, name=f"y{b}", tag=f"y{b}")
+            quantise_values(b)
+            if b == 1:
+                nc.vector.reciprocal(inv_total[:], total[:])
+            w_code.append(sb.tile([P, P], U32, name=f"w_code{b}", align_bytes=64))
+            w_scale.append(sb.tile([P, P], U8, name=f"w_scale{b}", align_bytes=64))
+            nc.vector.quantize_mx(w_code[b][:].bitcast(FP8X4), w_scale[b][:], w_woven[:].rearrange("s q t -> s (q t)"))
+        for b in range(QBLOCKS):
+            y.append(ps.tile([P, DV], F32, name=f"y{b}", tag=f"y{b}"))
             nc.tensor.matmul_mx(
-                y[:], lhsT=w_code[:].bitcast(FP8X4), lhsT_scale=w_scale[:],
+                y[b][:], lhsT=w_code[b][:].bitcast(FP8X4), lhsT_scale=w_scale[b][:],
                 rhs=v_code[:].bitcast(FP8X4), rhs_scale=v_scale[:], start=True, stop=True,
             )
+        for b in range(QBLOCKS):
             result = sb.tile([P, DV], F32, name=f"result{b}")
-            nc.vector.scalar_tensor_tensor(result[:], y[:], inv_total[:], gate[:, b, :], ALU.mult, ALU.mult)
-            nc.sync.dma_start(out[0, b * P : (b + 1) * P, :], result[:])
+            nc.vector.scalar_tensor_tensor(result[:], y[b][:], inv_total[:, b : b + 1], gate[:, b, :], ALU.mult, ALU.mult)
+            (nc.sync, nc.scalar)[b].dma_start(out[0, b * P : (b + 1) * P, :], result[:])

from contextlib import ExitStack

import concourse.mybir as mybir
from concourse.masks import make_identity

F32 = mybir.dt.float32
BF16 = mybir.dt.bfloat16
I32 = mybir.dt.int32
U32 = mybir.dt.uint32
U16 = mybir.dt.uint16
U8 = mybir.dt.uint8
FP8X4 = mybir.dt.float8_e4m3fn_x4
FP4X4 = mybir.dt.float4_e2m1fn_x4
ACT = mybir.ActivationFunctionType
ALU = mybir.AluOpType

N, T, D, DV, NQ = 512, 1024, 1024, 256, 256
P = 128
PACK = 4
PASSES = D // (P * PACK)
QBLOCKS = NQ // P
VHALVES = DV // P
SCALE_ROWS = 16
QUADS = 4

FLOPS = 2 * NQ * N * (D + DV)


def tile_attend_soft_sink_gate_srtq256n512t1024_kernel(tc, qT, k_words, k_scales, vT, vs, sink, og, offs, out):
    nc = tc.nc
    with ExitStack() as ctx:
        sb = ctx.enter_context(tc.tile_pool(name="sb", bufs=1))
        ps = ctx.enter_context(tc.psum_pool(name="ps", bufs=1))

        offsets = sb.tile([P, N // 16], U16, name="offsets")
        nc.sync.dma_start(offsets[:], offs)
        sink_rows = sb.tile([P, P], F32, name="sink_rows")
        nc.gpsimd.memset(sink_rows[: P - QBLOCKS, :], 0.0)
        nc.scalar.dma_start(sink_rows[P - QBLOCKS :, :], sink[0].rearrange("(b p) o -> b (p o)", p=P))
        first_row = P - PASSES * SCALE_ROWS
        ks_pool = sb.tile([P, T], U8, name="ks_pool", tag="pool0", align_bytes=64)
        nc.vector.memset(ks_pool[:first_row, :].bitcast(I32), 0)
        nc.sync.dma_start(ks_pool[first_row:, :].bitcast(I32), k_scales.bitcast(I32).rearrange("o f t -> f o t"))
        vs_pool = sb.tile([P, T], F32, name="vs_pool", tag="pool1", align_bytes=64)
        nc.vector.memset(vs_pool[: P - 1, :], 0.0)
        nc.sync.dma_start(vs_pool[P - 1 :, :], vs[0:1, :])
        kw_pool = sb.tile([P, T], U32, name="kw_pool", tag="pool2")
        nc.sync.dma_start(kw_pool[:].bitcast(I32), k_words[0].rearrange("p t b -> p (t b)").bitcast(I32))
        q_raw = []
        for g in range(PASSES):
            t_ = sb.tile([P, PACK, NQ], F32, name=f"q_raw{g}", tag=f"raw{g}", align_bytes=64)
            nc.sync.dma_start(t_[:], qT[0, g * P * PACK : (g + 1) * P * PACK, :].rearrange("(p j) q -> p j q", j=PACK))
            q_raw.append(t_)
        k_scale = sb.tile([P, PASSES, N], U8, name="k_scale", align_bytes=64)
        nc.gpsimd.memset(k_scale[:].rearrange("p o n -> p (o n)").bitcast(I32), 0)
        ident = sb.tile([P, P], F32, name="ident")
        make_identity(nc, ident[:])

        sink_turned = ps.tile([P, P], F32, name="sink_turned", tag="y0")
        nc.tensor.transpose(sink_turned[:], sink_rows[:], ident[:])
        sink_cols = sink_turned[:, P - QBLOCKS :]
        shared = sb.tile([P, 2 * N], BF16, name="shared", align_bytes=64)
        neg_score, neg_sink = [], []
        for b in range(QBLOCKS):
            t_ = sb.tile([P, N + 1], F32, name=f"neg_score{b}", tag=f"neg_score{b}", align_bytes=64)
            nc.scalar.activation(t_[:, N : N + 1], sink_cols[:, b : b + 1], ACT.Copy, scale=-1.0)
            neg_score.append(t_)
            if b == 0:
                neg_sink.append(t_[:, N : N + 1])
            else:
                neg_sink.append(shared[:, N : N + 2].bitcast(F32))
                nc.scalar.activation(neg_sink[b], sink_cols[:, b : b + 1], ACT.Copy, scale=-1.0)

        ks_got = sb.tile([P, N], U8, name="ks_got")
        nc.vector.tensor_copy(ks_got[:], ks_pool[:].indirect(offsets[:]))
        rows = PASSES * SCALE_ROWS // QUADS
        for quad in range(QUADS):
            nc.sync.dma_start(
                k_scale[32 * quad : 32 * quad + 4, :, :].bitcast(I32),
                ks_got[first_row + rows * quad : first_row + rows * (quad + 1), :].bitcast(I32),
            )
        vs_got = sb.tile([P, N], F32, name="vs_got")
        nc.vector.tensor_copy(vs_got[:], vs_pool[:].indirect(offsets[:]))
        vs_turned = ps.tile([P, PACK, P], F32, name="vs_turned", tag="y1")
        for t in range(PACK):
            nc.tensor.transpose(vs_turned[:, t, :], vs_got[:, t::PACK], ident[:])
        kw_got = sb.tile([P, N], U32, name="kw_got")
        nc.vector.tensor_copy(kw_got[:], kw_pool[:].indirect(offsets[:]))
        k_code = sb.tile([P, PASSES, 2 * N], U8, name="k_code", align_bytes=64)
        nc.vector.tensor_copy(k_code[:].bitcast(U16), kw_got[:].bitcast(U16).rearrange("p (n o) -> p o n", o=PASSES))

        v_pool = []
        for h in range(VHALVES):
            t_ = sb.tile([P, T], F32, name=f"v_pool{h}", tag=f"pool{h}", align_bytes=64)
            nc.sync.dma_start(t_[:], vT[h * P : (h + 1) * P, :])
            v_pool.append(t_)

        q_woven, q_code, q_scale = {}, {}, {}
        for g in range(PASSES):
            for b in range(QBLOCKS):
                if (g, b) == (1, 1):
                    q_woven[g, b] = shared[:, :N]
                else:
                    q_woven[g, b] = sb.tile([P, N], BF16, name=f"q_woven{g}{b}", align_bytes=64)[:]
                nc.scalar.activation(
                    q_woven[g, b].rearrange("p (c i t) -> p c t i", i=4, t=PACK),
                    q_raw[g][:, :, b * P : (b + 1) * P].rearrange("p t (c i) -> p c t i", i=4),
                    ACT.Copy,
                )
        for b in range(QBLOCKS):
            for g in range(PASSES):
                q_code[g, b] = sb.tile([P, P], U32, name=f"q_code{g}{b}", align_bytes=64)
                q_scale[g, b] = sb.tile([P, P], U8, name=f"q_scale{g}{b}", align_bytes=64)
                nc.vector.quantize_mx(q_code[g, b][:].bitcast(FP8X4), q_scale[g, b][:], q_woven[g, b])
        vs_col = sb.tile([P, PACK], F32, name="vs_col")
        nc.scalar.copy(vs_col[:], vs_turned[:, :, P - 1])
        og_sb = sb.tile([P, QBLOCKS, DV], F32, name="og_sb", tag="pool2")
        nc.sync.dma_start(og_sb[:], og[0].rearrange("(b p) e -> p b e", p=P))

        p_turned = []
        total = sb.tile([P, QBLOCKS], F32, name="total")
        for b in range(QBLOCKS):
            score = ps.tile([P, N], F32, name=f"score{b}", tag=f"score{b}")
            for g in range(PASSES):
                nc.tensor.matmul_mx(
                    score[:], lhsT=q_code[g, b][:].bitcast(FP8X4), lhsT_scale=q_scale[g, b][:],
                    rhs=k_code[:, g, :].bitcast(FP4X4), rhs_scale=k_scale[:, g, :],
                    start=(g == 0), stop=(g == PASSES - 1),
                )
            neg_max = sb.tile([P, 1], F32, name=f"neg_max{b}")
            nc.vector.tensor_scalar(
                neg_score[b][:, :N].rearrange("q (t s) -> q t s", t=PACK),
                score[:].rearrange("q (s t) -> q t s", t=PACK),
                -1.0, neg_sink[b], ALU.mult, ALU.min, accum_out=neg_max[:],
            )
            prob = sb.tile([P, N + 1], F32, name=f"prob{b}")
            nc.scalar.activation(prob[:], neg_score[b][:], ACT.Exp, bias=neg_max[:], scale=-1.0, accum_out=total[:, b : b + 1])
            turned = ps.tile([P, PACK, P], F32, name=f"p_turned{b}")
            for t in range(PACK):
                nc.tensor.transpose(turned[:, t, :], prob[:, t * P : (t + 1) * P], ident[:])
            p_turned.append(turned)


        half_tanh = sb.tile([P, QBLOCKS, DV], F32, name="half_tanh", tag="neg_score1", align_bytes=64)
        nc.scalar.activation(half_tanh[:], og_sb[:], ACT.Tanh, scale=0.5)
        gate = sb.tile([P, QBLOCKS, DV], F32, name="gate")
        nc.scalar.activation(gate[:], half_tanh[:], ACT.Copy, scale=0.5, bias=0.5)

        v_wovens = []
        for h in (0, 1):
            if h == 0:
                v_got = shared[:, N // 2 : N // 2 + N]
                for part in range(2):
                    nc.vector.tensor_copy(v_got[:, part * 256 : (part + 1) * 256], v_pool[h][:].indirect(offsets[:, 16 * part : 16 * (part + 1)]))
            else:
                v_got = sb.tile([P, N], BF16, name=f"v_got{h}", tag="pool0", align_bytes=64)[:]
                nc.vector.tensor_copy(v_got, v_pool[h][:].indirect(offsets[:]))
            v_turned = ps.tile([P, 2, P], F32, name=f"v_turned{h}")
            pairs = v_got.bitcast(F32)
            for u in range(2):
                nc.tensor.transpose(v_turned[:, u, :], pairs[:, u::2], ident[:])
            v_woven = sb.tile([P, P, PACK], BF16, name=f"v_woven{h}", tag=("neg_score1", "vwoven1")[h], align_bytes=64)
            nc.scalar.copy(v_woven[:].bitcast(F32), v_turned[:].rearrange("s u e -> s e u"))
            v_wovens.append(v_woven)

        v_code = sb.tile([P, DV], U32, name="v_code", align_bytes=64)
        v_scale = sb.tile([P, DV], U8, name="v_scale", align_bytes=64)
        inv_total = sb.tile([P, QBLOCKS], F32, name="inv_total")

        def quantise_values(h):
            nc.vector.quantize_mx(
                v_code[:, h * P : (h + 1) * P].bitcast(FP8X4), v_scale[:, h * P : (h + 1) * P],
                v_wovens[h][:].rearrange("s e t -> s (e t)"),
            )

        y, w_code, w_scale = [], [], []
        for b in range(QBLOCKS):
            w_woven = sb.tile([P, P, PACK], BF16, name=f"w_woven{b}", tag=("pool1", "wwoven1")[b], align_bytes=64)
            nc.vector.tensor_tensor(
                w_woven[:], p_turned[b][:].rearrange("s t q -> s q t"),
                vs_col[:].unsqueeze(1).to_broadcast([P, P, PACK]), ALU.mult,
            )
            quantise_values(b)
            if b == 1:
                nc.vector.reciprocal(inv_total[:], total[:])
            w_code.append(sb.tile([P, P], U32, name=f"w_code{b}", align_bytes=64))
            w_scale.append(sb.tile([P, P], U8, name=f"w_scale{b}", align_bytes=64))
            nc.vector.quantize_mx(w_code[b][:].bitcast(FP8X4), w_scale[b][:], w_woven[:].rearrange("s q t -> s (q t)"))
        for b in range(QBLOCKS):
            y.append(ps.tile([P, DV], F32, name=f"y{b}", tag=f"y{b}"))
            nc.tensor.matmul_mx(
                y[b][:], lhsT=w_code[b][:].bitcast(FP8X4), lhsT_scale=w_scale[b][:],
                rhs=v_code[:].bitcast(FP8X4), rhs_scale=v_scale[:], start=True, stop=True,
            )
        for b in range(QBLOCKS):
            result = sb.tile([P, DV], F32, name=f"result{b}")
            nc.vector.scalar_tensor_tensor(result[:], y[b][:], inv_total[:, b : b + 1], gate[:, b, :], ALU.mult, ALU.mult)
            (nc.sync, nc.scalar)[b].dma_start(out[0, b * P : (b + 1) * P, :], result[:])
